import numpy as np
import ml_dtypes


def mxq(x, axis, fmt="e4m3"):
    dtype, down = {"e4m3": (ml_dtypes.float8_e4m3fn, 7), "e5m2": (ml_dtypes.float8_e5m2, 14)}[fmt]
    v = np.moveaxis(np.asarray(x, np.float32).astype(ml_dtypes.bfloat16).astype(np.float64), axis, -1)
    blocks = v.reshape(v.shape[:-1] + (-1, 32))
    amax = np.abs(blocks).max(-1, keepdims=True)
    byte = np.maximum(np.where(amax > 0, np.frexp(amax)[1] - 1 + 127, 0) - down, 1)
    scale = np.exp2(byte - 127.0)
    codes = (blocks / scale).astype(np.float32).astype(dtype).astype(np.float64)
    return np.moveaxis((codes * scale).reshape(v.shape), -1, axis)


WIDE = False


def mx_kscale(k):
    if not WIDE:
        return np.ones(k)
    levels = np.array([30, -30])
    if k % 512:
        return np.exp2(np.random.permutation(np.resize(levels, k // 32))).repeat(32)
    a = np.empty((k // 512, 16))
    for p in range(k // 512):
        a[p, :8] = np.random.permutation(np.resize(levels, 8))
        for g in range(8):
            far = levels[np.abs(levels - a[p, g]) >= 10]
            a[p, g + 8] = far[np.random.randint(len(far))]
    return np.exp2(a.ravel()).repeat(32)


def f64(x):
    return np.asarray(x).astype(np.float64)


def striped(idx):
    return np.tile(np.asarray(idx).reshape(-1, 16).T, (8, 1)).astype(np.uint16)


def unstriped(offs):
    return offs[:16].T.reshape(-1).astype(np.int64)


E2M1 = np.array([0.0, 0.5, 1.0, 1.5, 2.0, 3.0, 4.0, 6.0, -0.0, -0.5, -1.0, -1.5, -2.0, -3.0, -4.0, -6.0])


def pack_weight(w, fmt):
    k, n = w.shape
    w = f64(np.asarray(w, np.float32).astype(ml_dtypes.bfloat16)).reshape(k // 32, 32, n)
    amax = np.abs(w).max(1)
    if fmt in ("e4m3", "e5m2"):
        byte = np.frexp(amax)[1] - 1 + 127 - (7 if fmt == "e4m3" else 14)
    else:
        mant, ex = np.frexp(amax / 6.0)
        byte = np.where(mant > 0.5, ex, ex - 1) + 127
    byte = np.clip(np.where(amax > 0, byte, 1), 1, 254)
    scaled = (w * np.exp2(127.0 - byte)[:, None, :]).reshape(k, n).astype(np.float32)
    by_word = np.ascontiguousarray(scaled.reshape(k // 512, 128, 4, n).transpose(0, 1, 3, 2))
    if fmt in ("e4m3", "e5m2"):
        words = by_word.astype(ml_dtypes.float8_e4m3fn if fmt == "e4m3" else ml_dtypes.float8_e5m2).view(np.uint8)
    else:
        c = by_word.astype(ml_dtypes.float4_e2m1fn).view(np.uint8) & 0xF
        words = (c[..., 0::2] | (c[..., 1::2] << 4)).reshape(k // 512, 128, 2 * n)
    return np.ascontiguousarray(words), np.ascontiguousarray(byte.astype(np.uint8).reshape(k // 512, 16, n))


def unpack_weight(words, scales, fmt):
    g, _, n = scales.shape
    words = np.ascontiguousarray(words).reshape(g, 128, n, -1)
    if fmt in ("e4m3", "e5m2"):
        vals = words.view(ml_dtypes.float8_e4m3fn if fmt == "e4m3" else ml_dtypes.float8_e5m2).astype(np.float64)
    else:
        nib = np.empty((g, 128, n, 4), np.uint8)
        nib[..., 0::2] = words & 0xF
        nib[..., 1::2] = words >> 4
        vals = E2M1[nib]
    vals = vals * np.repeat(np.exp2(scales.astype(np.float64) - 127.0), 8, axis=1)[..., None]
    return vals.transpose(0, 1, 3, 2).reshape(g * 512, n)


K, T, J, R, F, N = 512, 512, 256, 512, 512, 256


def setup_inputs():
    n = np.random.standard_normal
    idx = np.random.permutation(T)[:J]
    idx2 = np.random.permutation(T)[:J]
    fk = mx_kscale(K)
    fr = mx_kscale(R)
    ff = mx_kscale(F)
    wp = pack_weight(n((K, R)) * 1 / np.sqrt(K) * fk[:, None] * fr, "e2m1")
    sxp = pack_weight(n((F, J)) / ff[:, None], "e4m3")
    w2p = pack_weight(n((F, R)) * 1 / np.sqrt(F) * ff[:, None] * fr, "e5m2")
    wbp = pack_weight(n((R, N)) * 1 / np.sqrt(R) / fr[:, None], "e5m2")
    return {
        "xf": (n((K, T))).astype(np.float32),
        "fk": (np.random.uniform(0.5, 2.0, (K, 1)) / fk[:, None]).astype(np.float32),
        "w_words": wp[0],
        "w_scales": wp[1],
        "sx_words": sxp[0],
        "sx_scales": sxp[1],
        "w2_words": w2p[0],
        "w2_scales": w2p[1],
        "wb_words": wbp[0],
        "wb_scales": wbp[1],
        "rs": (1.0 * n((J, N))).astype(np.float32),
        "offs": striped(idx),
        "offs2": striped(idx2),
    }


def reference(xf, fk, w_words, w_scales, sx_words, sx_scales, w2_words, w2_scales, wb_words, wb_scales, rs, offs, offs2):
    idx = unstriped(offs)
    idx2 = unstriped(offs2)
    wu = unpack_weight(w_words, w_scales, "e2m1")
    sxu = unpack_weight(sx_words, sx_scales, "e4m3")
    w2u = unpack_weight(w2_words, w2_scales, "e5m2")
    wbu = unpack_weight(wb_words, wb_scales, "e5m2")
    u = np.maximum(f64(xf)[:, idx], f64(xf)[:, idx2]) * f64(fk)
    uq = mxq(u, 0, "e4m3")
    a = wu.T @ uq + w2u.T @ sxu
    ha = np.maximum(a, 0.0)
    h1 = np.pad(ha, ((0, 0), (2, 0)))[:, :J]
    hid = ha - 0.5 * h1
    hidq = mxq(hid, 0, "e5m2")
    p = hidq.T @ wbu
    mn = np.mean(np.abs(p), axis=1, keepdims=True)
    y = np.maximum(p - mn, 0.0) - 0.3 * f64(rs)
    return y

@@ -1,0 +1,192 @@
+from contextlib import ExitStack
+
+import concourse.mybir as mybir
+
+K, T, J, R, F, N = 512, 512, 256, 512, 512, 256
+FLOPS = 2 * K * R * J + 2 * F * R * J + 2 * R * J * N
+
+F32 = mybir.dt.float32
+BF16 = mybir.dt.bfloat16
+I32 = mybir.dt.int32
+U32 = mybir.dt.uint32
+U16 = mybir.dt.uint16
+U8 = mybir.dt.uint8
+E4M3 = mybir.dt.float8_e4m3fn_x4
+E5M2 = mybir.dt.float8_e5m2_x4
+E2M1 = mybir.dt.float4_e2m1fn_x4
+ALU = mybir.AluOpType
+ACT = mybir.ActivationFunctionType
+
+P = 128
+PACK = 4
+H = 128
+HALVES = J // H
+LAG = 2
+
+
+def load_scales(queue, plane, scales, quadrants=range(4)):
+    for q in quadrants:
+        queue.dma_start(out=plane[32 * q : 32 * q + 4, :].bitcast(I32), in_=scales[0, 4 * q : 4 * q + 4, :].bitcast(I32))
+
+
+def dealt(src, dst, run):
+    return (
+        dst.rearrange("p (t c i) -> p c t i", t=PACK, i=run),
+        src.rearrange("p (c i t) -> p c t i", t=PACK, i=run),
+    )
+
+
+def tile_list_sum_largerpicks_own_lagged_rowabove_kernel(
+    tc, xf, fk, w_words, w_scales, sx_words, sx_scales, w2_words, w2_scales, wb_words, wb_scales, rs, offs, offs2, out
+):
+    nc = tc.nc
+    with ExitStack() as ctx:
+        keep = ctx.enter_context(tc.tile_pool(name="keep", bufs=1))
+        psum = ctx.enter_context(tc.psum_pool(name="psum", bufs=1))
+
+        list_a = keep.tile([P, J // 16], U16, name="list_a")
+        list_b = keep.tile([P, J // 16], U16, name="list_b")
+        planes = [keep.tile([P, T], F32, name="plane%d" % t) for t in range(PACK)]
+        fk_t = keep.tile([P, PACK], F32, name="fk_t")
+        w_raw = keep.tile([P, R], U16, name="w_raw", align_bytes=64)
+        w2_raw = keep.tile([P, R], U32, name="w2_raw", align_bytes=64)
+        ws_raw = keep.tile([P, R], U8, name="ws_raw", align_bytes=64)[:]
+        w2s_raw = keep.tile([P, R], U8, name="w2s_raw", align_bytes=64)[:]
+        sx_s = keep.tile([P, J], U8, name="sx_s", align_bytes=64)[:]
+        wb_s = keep.tile([P, N], U8, name="wb_s", align_bytes=64)[:]
+        w_c = keep.tile([P, R], U16, name="w_c", align_bytes=64)
+        w2_c = keep.tile([P, R], U32, name="w2_c", align_bytes=64)
+        w_s = keep.tile([P, R], U8, name="w_s", align_bytes=64)
+        w2_s = keep.tile([P, R], U8, name="w2_s", align_bytes=64)
+        sx_c = keep.tile([P, J], U32, name="sx_c", align_bytes=64)
+        wb_c = keep.tile([P, N], U32, name="wb_c", align_bytes=64)
+        rs_t = keep.tile([P, HALVES, N], F32, name="rs_t")
+
+        for plane in (ws_raw, w2s_raw, sx_s):
+            nc.vector.memset(plane.bitcast(I32), 0)
+        nc.gpsimd.memset(wb_s.bitcast(I32), 0)
+        x_rows = xf.rearrange("(p t) c -> p t c", t=PACK)
+        nc.sync.dma_start(list_a[:], offs)
+        nc.sync.dma_start(list_b[:], offs2)
+        for t in range(PACK):
+            nc.sync.dma_start(out=planes[t][:], in_=x_rows[:, t, :])
+        nc.gpsimd.dma_start(out=fk_t[:], in_=fk.rearrange("(p t) o -> p (t o)", t=PACK))
+        load_scales(nc.gpsimd, wb_s, wb_scales)
+        load_scales(nc.sync, ws_raw, w_scales)
+        load_scales(nc.sync, w2s_raw, w2_scales, range(0, 1))
+        nc.sync.dma_start(out=w2_raw[:].bitcast(I32), in_=w2_words[0].rearrange("p n t -> p (n t)").bitcast(I32))
+        nc.sync.dma_start(out=w_raw[:].bitcast(I32), in_=w_words[0].bitcast(I32))
+        load_scales(nc.sync, w2s_raw, w2_scales, range(1, 4))
+        nc.sync.dma_start(out=sx_c[:].bitcast(I32), in_=sx_words[0].rearrange("p n t -> p (n t)").bitcast(I32))
+        load_scales(nc.sync, sx_s, sx_scales)
+        nc.sync.dma_start(out=wb_c[:].bitcast(I32), in_=wb_words[0].rearrange("p n t -> p (n t)").bitcast(I32))
+        nc.sync.dma_start(out=rs_t[:], in_=rs.rearrange("(h p) n -> p h n", p=P))
+
+        ha = keep.tile([P, (LAG + J) * PACK], F32, name="ha")
+        nc.vector.memset(ha[:, 0 : LAG * PACK], 0.0)
+
+        pick_a = keep.tile([P, PACK, J], F32, name="pick_a")
+        pick_b = keep.tile([P, PACK, J], F32, name="pick_b")
+        larger = keep.tile([P, PACK, J], F32, name="larger")
+
+        def gather(on_vector, picks, offsets, t, lo, hi):
+            window = planes[t][:].indirect(offsets[:, lo // 16 : hi // 16])
+            if on_vector:
+                nc.vector.tensor_copy(picks[:, t, lo:hi], window)
+            else:
+                nc.scalar.activation(picks[:, t, lo:hi], window, ACT.Copy)
+
+        def keep_larger(pair, cols):
+            nc.vector.tensor_tensor(larger[:, pair, cols], pick_a[:, pair, cols], pick_b[:, pair, cols], ALU.max)
+
+        for t in (0, 1):
+            gather(False, pick_a, list_a, t, 0, J)
+            gather(True, pick_b, list_b, t, 0, J)
+        keep_larger(slice(0, 2), slice(0, J))
+        for t in (2, 3):
+            gather(t == 3, pick_a, list_a, t, 0, H)
+            gather(t == 3, pick_b, list_b, t, 0, H)
+        for t in (2, 3):
+            gather(False, pick_a, list_a, t, H, J)
+            gather(False, pick_b, list_b, t, H, J)
+
+        u_b = [keep.tile([P, H, PACK], BF16, name="u_b%d" % h, align_bytes=64) for h in range(HALVES)]
+        u_c = [keep.tile([P, H], U32, name="u_c%d" % h, align_bytes=64) for h in range(HALVES)]
+        u_s = [keep.tile([P, H], U8, name="u_s%d" % h, align_bytes=64) for h in range(HALVES)]
+        fk_wide = fk_t[:].unsqueeze(1).unsqueeze(3).to_broadcast([P, H // 4, PACK, 4])
+
+        def make_u(h):
+            cols = slice(h * H, (h + 1) * H)
+            keep_larger(slice(2, 4), cols)
+            nc.vector.tensor_tensor(
+                u_b[h][:].rearrange("p (c i) t -> p c t i", i=4),
+                larger[:, :, cols].rearrange("p t (c i) -> p c t i", i=4),
+                fk_wide,
+                ALU.mult,
+            )
+            nc.vector.quantize_mx(out=u_c[h][:].bitcast(E4M3), scales=u_s[h][:], in_=u_b[h][:].rearrange("p j t -> p (j t)"))
+
+        make_u(0)
+        nc.scalar.copy(*dealt(w2_raw[:], w2_c[:], 4))
+        nc.scalar.copy(*dealt(w_raw[:], w_c[:], 8))
+        nc.vector.tensor_copy(*dealt(w2s_raw, w2_s[:], 16))
+        nc.vector.tensor_copy(*dealt(ws_raw, w_s[:], 16))
+        make_u(1)
+
+        sums = [psum.tile([P, PACK, H], F32, name="sums%d" % h) for h in range(HALVES)]
+        for h in range(HALVES):
+            cols = slice(h * H, (h + 1) * H)
+            for t in range(PACK):
+                rows = slice(t * P, (t + 1) * P)
+                nc.tensor.matmul_mx(
+                    out=sums[h][:, t, :],
+                    lhsT=w2_c[:, rows].bitcast(E5M2),
+                    lhsT_scale=w2_s[:, rows],
+                    rhs=sx_c[:, cols].bitcast(E4M3),
+                    rhs_scale=sx_s[:, cols],
+                    start=(t == 0),
+                    stop=False,
+                )
+        hid_b = [keep.tile([P, H * PACK], BF16, name="hid_b%d" % h, align_bytes=64) for h in range(HALVES)]
+        hid_c = [keep.tile([P, H], U32, name="hid_c%d" % h, align_bytes=64) for h in range(HALVES)]
+        hid_s = [keep.tile([P, H], U8, name="hid_s%d" % h, align_bytes=64) for h in range(HALVES)]
+        for h in range(HALVES):
+            for t in range(PACK):
+                rows = slice(t * P, (t + 1) * P)
+                nc.tensor.matmul_mx(
+                    out=sums[h][:, t, :],
+                    lhsT=w_c[:, rows].bitcast(E2M1),
+                    lhsT_scale=w_s[:, rows],
+                    rhs=u_c[h][:].bitcast(E4M3),
+                    rhs_scale=u_s[h][:],
+                    start=False,
+                    stop=(t == PACK - 1),
+                )
+            first = h * H * PACK
+            now = ha[:, first + LAG * PACK : first + (LAG + H) * PACK]
+            nc.scalar.activation(now.rearrange("p (j t) -> p j t", t=PACK), sums[h][:].rearrange("p t j -> p j t"), ACT.Relu)
+        prod = [psum.tile([P, N], F32, name="prod%d" % h) for h in range(HALVES)]
+        for h in range(HALVES):
+            first = h * H * PACK
+            now = ha[:, first + LAG * PACK : first + (LAG + H) * PACK]
+            before = ha[:, first : first + H * PACK]
+            nc.vector.scalar_tensor_tensor(hid_b[h][:], before, -0.5, now, ALU.mult, ALU.add)
+            nc.vector.quantize_mx(out=hid_c[h][:].bitcast(E5M2), scales=hid_s[h][:], in_=hid_b[h][:])
+            nc.tensor.matmul_mx(
+                out=prod[h][:],
+                lhsT=hid_c[h][:].bitcast(E5M2),
+                lhsT_scale=hid_s[h][:],
+                rhs=wb_c[:].bitcast(E5M2),
+                rhs_scale=wb_s,
+                start=True,
+                stop=True,
+            )
+        for h in range(HALVES):
+            size = keep.tile([P, N], F32, name="size%d" % h)
+            mean = keep.tile([P, 1], F32, name="mean%d" % h)
+            taken = keep.tile([P, N], F32, name="taken%d" % h)
+            result = keep.tile([P, N], F32, name="result%d" % h)
+            nc.scalar.activation(size[:], prod[h][:], ACT.Abs, scale=1.0 / N, accum_out=mean[:])
+            nc.vector.tensor_scalar(taken[:], rs_t[:, h, :], 0.3, mean[:], ALU.mult, ALU.add)
+            nc.vector.scalar_tensor_tensor(result[:], prod[h][:], mean[:], taken[:], ALU.max, ALU.subtract)
+            nc.sync.dma_start(out=out[h * H : (h + 1) * H, :], in_=result[:])

@@ -46,12 +46,15 @@ def tile_list_sum_largerpicks_own_lagged_rowabove_kernel(
 
         list_a = keep.tile([P, J // 16], U16, name="list_a")
         list_b = keep.tile([P, J // 16], U16, name="list_b")
-        planes = [keep.tile([P, T], F32, name="plane%d" % t) for t in range(PACK)]
+        x0 = keep.tile([P, T], F32, name="x0")
+        x1 = keep.tile([P, T], F32, name="x1")
+        x23 = keep.tile([P, 2, T], F32, name="x23")
+        planes = [x0[:], x1[:], x23[:, 0, :], x23[:, 1, :]]
         fk_t = keep.tile([P, PACK], F32, name="fk_t")
-        w_raw = keep.tile([P, R], U16, name="w_raw", align_bytes=64)
-        w2_raw = keep.tile([P, R], U32, name="w2_raw", align_bytes=64)
+        w_raw = keep.tile([P, R], U16, name="w_raw", tag="w_then_a", align_bytes=64)
+        w2_raw = keep.tile([P, R], U32, name="w2_raw", tag="w2_then_b", align_bytes=64)
         ws_raw = keep.tile([P, R], U8, name="ws_raw", align_bytes=64)[:]
-        w2s_raw = keep.tile([P, R], U8, name="w2s_raw", align_bytes=64)[:]
+        w2s_raw = keep.tile([P, R], U8, name="w2s_raw", tag="w2s_then_u", align_bytes=64)[:]
         sx_s = keep.tile([P, J], U8, name="sx_s", align_bytes=64)[:]
         wb_s = keep.tile([P, N], U8, name="wb_s", align_bytes=64)[:]
         w_c = keep.tile([P, R], U16, name="w_c", align_bytes=64)
@@ -63,74 +66,72 @@ def tile_list_sum_largerpicks_own_lagged_rowabove_kernel(
         rs_t = keep.tile([P, HALVES, N], F32, name="rs_t")
 
         for plane in (ws_raw, w2s_raw, sx_s):
-            nc.vector.memset(plane.bitcast(I32), 0)
-        nc.gpsimd.memset(wb_s.bitcast(I32), 0)
+            nc.gpsimd.memset(plane.bitcast(I32), 0)
+        nc.vector.memset(wb_s.bitcast(I32), 0)
         x_rows = xf.rearrange("(p t) c -> p t c", t=PACK)
+        nc.sync.dma_start(out=x0[:], in_=x_rows[:, 0, :])
         nc.sync.dma_start(list_a[:], offs)
         nc.sync.dma_start(list_b[:], offs2)
-        for t in range(PACK):
-            nc.sync.dma_start(out=planes[t][:], in_=x_rows[:, t, :])
+        nc.sync.dma_start(out=x1[:], in_=x_rows[:, 1, :])
+        load_scales(nc.sync, ws_raw, w_scales, range(0, 3))
+        nc.sync.dma_start(out=x23[:], in_=x_rows[:, 2:4, :])
         nc.gpsimd.dma_start(out=fk_t[:], in_=fk.rearrange("(p t) o -> p (t o)", t=PACK))
-        load_scales(nc.gpsimd, wb_s, wb_scales)
-        load_scales(nc.sync, ws_raw, w_scales)
-        load_scales(nc.sync, w2s_raw, w2_scales, range(0, 1))
-        nc.sync.dma_start(out=w2_raw[:].bitcast(I32), in_=w2_words[0].rearrange("p n t -> p (n t)").bitcast(I32))
+        load_scales(nc.gpsimd, sx_s, sx_scales)
         nc.sync.dma_start(out=w_raw[:].bitcast(I32), in_=w_words[0].bitcast(I32))
-        load_scales(nc.sync, w2s_raw, w2_scales, range(1, 4))
+        nc.sync.dma_start(out=w2_raw[:].bitcast(I32), in_=w2_words[0].rearrange("p n t -> p (n t)").bitcast(I32))
+        load_scales(nc.sync, ws_raw, w_scales, range(3, 4))
+        load_scales(nc.sync, w2s_raw, w2_scales)
         nc.sync.dma_start(out=sx_c[:].bitcast(I32), in_=sx_words[0].rearrange("p n t -> p (n t)").bitcast(I32))
-        load_scales(nc.sync, sx_s, sx_scales)
         nc.sync.dma_start(out=wb_c[:].bitcast(I32), in_=wb_words[0].rearrange("p n t -> p (n t)").bitcast(I32))
+        load_scales(nc.sync, wb_s, wb_scales)
         nc.sync.dma_start(out=rs_t[:], in_=rs.rearrange("(h p) n -> p h n", p=P))
 
         ha = keep.tile([P, (LAG + J) * PACK], F32, name="ha")
-        nc.vector.memset(ha[:, 0 : LAG * PACK], 0.0)
+        zeros = keep.tile([P, LAG * PACK], F32, name="zeros")
+        nc.vector.memset(zeros[:], 0.0)
+        nc.scalar.activation(ha[:, 0 : LAG * PACK], zeros[:], ACT.Relu)
 
-        pick_a = keep.tile([P, PACK, J], F32, name="pick_a")
-        pick_b = keep.tile([P, PACK, J], F32, name="pick_b")
         larger = keep.tile([P, PACK, J], F32, name="larger")
 
-        def gather(on_vector, picks, offsets, t, lo, hi):
-            window = planes[t][:].indirect(offsets[:, lo // 16 : hi // 16])
+        def gather(on_vector, pick, offsets, t, cols):
+            window = planes[t].indirect(offsets[:, cols.start // 16 : cols.stop // 16])
             if on_vector:
-                nc.vector.tensor_copy(picks[:, t, lo:hi], window)
+                nc.vector.tensor_copy(pick, window)
             else:
-                nc.scalar.activation(picks[:, t, lo:hi], window, ACT.Copy)
+                nc.scalar.activation(pick, window, ACT.Copy)
 
-        def keep_larger(pair, cols):
-            nc.vector.tensor_tensor(larger[:, pair, cols], pick_a[:, pair, cols], pick_b[:, pair, cols], ALU.max)
+        def pick_pair(first, cols, b_on_vector, tag_a, tag_b):
+            width = cols.stop - cols.start
+            pick_a = keep.tile([P, 2, width], F32, name="a" + tag_a, tag=tag_a, align_bytes=64)
+            pick_b = keep.tile([P, 2, width], F32, name="b" + tag_b, tag=tag_b, align_bytes=64)
+            for t in range(2):
+                gather(False, pick_a[:, t, :], list_a, first + t, cols)
+                gather(b_on_vector, pick_b[:, t, :], list_b, first + t, cols)
+            nc.vector.tensor_tensor(larger[:, first : first + 2, cols], pick_a[:], pick_b[:], ALU.max)
 
-        for t in (0, 1):
-            gather(False, pick_a, list_a, t, 0, J)
-            gather(True, pick_b, list_b, t, 0, J)
-        keep_larger(slice(0, 2), slice(0, J))
-        for t in (2, 3):
-            gather(t == 3, pick_a, list_a, t, 0, H)
-            gather(t == 3, pick_b, list_b, t, 0, H)
-        for t in (2, 3):
-            gather(False, pick_a, list_a, t, H, J)
-            gather(False, pick_b, list_b, t, H, J)
-
-        u_b = [keep.tile([P, H, PACK], BF16, name="u_b%d" % h, align_bytes=64) for h in range(HALVES)]
         u_c = [keep.tile([P, H], U32, name="u_c%d" % h, align_bytes=64) for h in range(HALVES)]
         u_s = [keep.tile([P, H], U8, name="u_s%d" % h, align_bytes=64) for h in range(HALVES)]
         fk_wide = fk_t[:].unsqueeze(1).unsqueeze(3).to_broadcast([P, H // 4, PACK, 4])
 
         def make_u(h):
             cols = slice(h * H, (h + 1) * H)
-            keep_larger(slice(2, 4), cols)
+            u_b = keep.tile([P, H, PACK], BF16, name="u_b%d" % h, tag=("u0", "w2s_then_u")[h], align_bytes=64)
             nc.vector.tensor_tensor(
-                u_b[h][:].rearrange("p (c i) t -> p c t i", i=4),
+                u_b[:].rearrange("p (c i) t -> p c t i", i=4),
                 larger[:, :, cols].rearrange("p t (c i) -> p c t i", i=4),
                 fk_wide,
                 ALU.mult,
             )
-            nc.vector.quantize_mx(out=u_c[h][:].bitcast(E4M3), scales=u_s[h][:], in_=u_b[h][:].rearrange("p j t -> p (j t)"))
+            nc.vector.quantize_mx(out=u_c[h][:].bitcast(E4M3), scales=u_s[h][:], in_=u_b[:].rearrange("p j t -> p (j t)"))
 
+        pick_pair(0, slice(0, J), True, "a01", "b01")
+        pick_pair(2, slice(0, H), True, "a23", "b23")
         make_u(0)
-        nc.scalar.copy(*dealt(w2_raw[:], w2_c[:], 4))
         nc.scalar.copy(*dealt(w_raw[:], w_c[:], 8))
-        nc.vector.tensor_copy(*dealt(w2s_raw, w2_s[:], 16))
+        nc.scalar.copy(*dealt(w2_raw[:], w2_c[:], 4))
         nc.vector.tensor_copy(*dealt(ws_raw, w_s[:], 16))
+        nc.vector.tensor_copy(*dealt(w2s_raw, w2_s[:], 16))
+        pick_pair(2, slice(H, J), False, "w_then_a", "w2_then_b")
         make_u(1)
 
         sums = [psum.tile([P, PACK, H], F32, name="sums%d" % h) for h in range(HALVES)]
@@ -147,10 +148,6 @@ def tile_list_sum_largerpicks_own_lagged_rowabove_kernel(
                     start=(t == 0),
                     stop=False,
                 )
-        hid_b = [keep.tile([P, H * PACK], BF16, name="hid_b%d" % h, align_bytes=64) for h in range(HALVES)]
-        hid_c = [keep.tile([P, H], U32, name="hid_c%d" % h, align_bytes=64) for h in range(HALVES)]
-        hid_s = [keep.tile([P, H], U8, name="hid_s%d" % h, align_bytes=64) for h in range(HALVES)]
-        for h in range(HALVES):
             for t in range(PACK):
                 rows = slice(t * P, (t + 1) * P)
                 nc.tensor.matmul_mx(
@@ -165,28 +162,35 @@ def tile_list_sum_largerpicks_own_lagged_rowabove_kernel(
             first = h * H * PACK
             now = ha[:, first + LAG * PACK : first + (LAG + H) * PACK]
             nc.scalar.activation(now.rearrange("p (j t) -> p j t", t=PACK), sums[h][:].rearrange("p t j -> p j t"), ACT.Relu)
-        prod = [psum.tile([P, N], F32, name="prod%d" % h) for h in range(HALVES)]
+        hid_b = [keep.tile([P, H * PACK], BF16, name="hid_b%d" % h, align_bytes=64) for h in range(HALVES)]
+        hid_c = [keep.tile([P, H], U32, name="hid_c%d" % h, align_bytes=64) for h in range(HALVES)]
+        hid_s = [keep.tile([P, H], U8, name="hid_s%d" % h, align_bytes=64) for h in range(HALVES)]
+        prod = [[psum.tile([P, N], F32, name="prod%d%d" % (h, r)) for r in range(2)] for h in range(HALVES)]
+        less = keep.tile([P, HALVES, N], F32, name="less")
+        for h in range(HALVES):
+            nc.scalar.activation(less[:, h, :], rs_t[:, h, :], ACT.Copy, scale=-0.3)
         for h in range(HALVES):
             first = h * H * PACK
             now = ha[:, first + LAG * PACK : first + (LAG + H) * PACK]
             before = ha[:, first : first + H * PACK]
             nc.vector.scalar_tensor_tensor(hid_b[h][:], before, -0.5, now, ALU.mult, ALU.add)
             nc.vector.quantize_mx(out=hid_c[h][:].bitcast(E5M2), scales=hid_s[h][:], in_=hid_b[h][:])
-            nc.tensor.matmul_mx(
-                out=prod[h][:],
-                lhsT=hid_c[h][:].bitcast(E5M2),
-                lhsT_scale=hid_s[h][:],
-                rhs=wb_c[:].bitcast(E5M2),
-                rhs_scale=wb_s,
-                start=True,
-                stop=True,
-            )
+            for bank in prod[h]:
+                nc.tensor.matmul_mx(
+                    out=bank[:],
+                    lhsT=hid_c[h][:].bitcast(E5M2),
+                    lhsT_scale=hid_s[h][:],
+                    rhs=wb_c[:].bitcast(E5M2),
+                    rhs_scale=wb_s,
+                    start=True,
+                    stop=True,
+                )
         for h in range(HALVES):
             size = keep.tile([P, N], F32, name="size%d" % h)
             mean = keep.tile([P, 1], F32, name="mean%d" % h)
             taken = keep.tile([P, N], F32, name="taken%d" % h)
             result = keep.tile([P, N], F32, name="result%d" % h)
-            nc.scalar.activation(size[:], prod[h][:], ACT.Abs, scale=1.0 / N, accum_out=mean[:])
-            nc.vector.tensor_scalar(taken[:], rs_t[:, h, :], 0.3, mean[:], ALU.mult, ALU.add)
-            nc.vector.scalar_tensor_tensor(result[:], prod[h][:], mean[:], taken[:], ALU.max, ALU.subtract)
+            nc.scalar.activation(size[:], prod[h][0][:], ACT.Abs, scale=1.0 / N, accum_out=mean[:])
+            nc.vector.tensor_tensor(taken[:], prod[h][1][:], less[:, h, :], ALU.add)
+            nc.vector.scalar_tensor_tensor(result[:], taken[:], mean[:], less[:, h, :], ALU.subtract, ALU.max)
             nc.sync.dma_start(out=out[h * H : (h + 1) * H, :], in_=result[:])

@@ -46,45 +46,39 @@ def tile_list_sum_largerpicks_own_lagged_rowabove_kernel(
 
         list_a = keep.tile([P, J // 16], U16, name="list_a")
         list_b = keep.tile([P, J // 16], U16, name="list_b")
-        x0 = keep.tile([P, T], F32, name="x0")
-        x1 = keep.tile([P, T], F32, name="x1")
-        x23 = keep.tile([P, 2, T], F32, name="x23")
-        planes = [x0[:], x1[:], x23[:, 0, :], x23[:, 1, :]]
+        planes = [keep.tile([P, T], F32, name="x%d" % t, tag="x%d" % t, align_bytes=64)[:] for t in range(PACK)]
         fk_t = keep.tile([P, PACK], F32, name="fk_t")
-        w_raw = keep.tile([P, R], U16, name="w_raw", tag="w_then_a", align_bytes=64)
-        w2_raw = keep.tile([P, R], U32, name="w2_raw", tag="w2_then_b", align_bytes=64)
-        ws_raw = keep.tile([P, R], U8, name="ws_raw", align_bytes=64)[:]
-        w2s_raw = keep.tile([P, R], U8, name="w2s_raw", tag="w2s_then_u", align_bytes=64)[:]
+        w_raw = keep.tile([P, R], U16, name="w_raw", align_bytes=64)
+        w2_raw = keep.tile([P, R], U32, name="w2_raw", tag="w2_then_a", align_bytes=64)
+        ws_raw = keep.tile([P, R], U8, name="ws_raw", tag="w2s_then_u", align_bytes=64)[:]
+        w2s_raw = keep.tile([P, R], U8, name="w2s_raw", align_bytes=64)[:]
         sx_s = keep.tile([P, J], U8, name="sx_s", align_bytes=64)[:]
         wb_s = keep.tile([P, N], U8, name="wb_s", align_bytes=64)[:]
-        w_c = keep.tile([P, R], U16, name="w_c", align_bytes=64)
-        w2_c = keep.tile([P, R], U32, name="w2_c", align_bytes=64)
         w_s = keep.tile([P, R], U8, name="w_s", align_bytes=64)
         w2_s = keep.tile([P, R], U8, name="w2_s", align_bytes=64)
         sx_c = keep.tile([P, J], U32, name="sx_c", align_bytes=64)
         wb_c = keep.tile([P, N], U32, name="wb_c", align_bytes=64)
         rs_t = keep.tile([P, HALVES, N], F32, name="rs_t")
 
-        for plane in (ws_raw, w2s_raw, sx_s):
-            nc.gpsimd.memset(plane.bitcast(I32), 0)
-        nc.vector.memset(wb_s.bitcast(I32), 0)
+        for plane in (w2s_raw, sx_s, ws_raw, wb_s):
+            nc.vector.memset(plane.bitcast(I32), 0)
         x_rows = xf.rearrange("(p t) c -> p t c", t=PACK)
-        nc.sync.dma_start(out=x0[:], in_=x_rows[:, 0, :])
+        nc.sync.dma_start(out=planes[0], in_=x_rows[:, 0, :])
         nc.sync.dma_start(list_a[:], offs)
         nc.sync.dma_start(list_b[:], offs2)
-        nc.sync.dma_start(out=x1[:], in_=x_rows[:, 1, :])
-        load_scales(nc.sync, ws_raw, w_scales, range(0, 3))
-        nc.sync.dma_start(out=x23[:], in_=x_rows[:, 2:4, :])
+        for t in range(1, PACK):
+            nc.sync.dma_start(out=planes[t], in_=x_rows[:, t, :])
         nc.gpsimd.dma_start(out=fk_t[:], in_=fk.rearrange("(p t) o -> p (t o)", t=PACK))
-        load_scales(nc.gpsimd, sx_s, sx_scales)
-        nc.sync.dma_start(out=w_raw[:].bitcast(I32), in_=w_words[0].bitcast(I32))
-        nc.sync.dma_start(out=w2_raw[:].bitcast(I32), in_=w2_words[0].rearrange("p n t -> p (n t)").bitcast(I32))
-        load_scales(nc.sync, ws_raw, w_scales, range(3, 4))
+        load_scales(nc.gpsimd, sx_s, sx_scales, range(0, 3))
         load_scales(nc.sync, w2s_raw, w2_scales)
+        nc.sync.dma_start(out=w2_raw[:].bitcast(I32), in_=w2_words[0].rearrange("p n t -> p (n t)").bitcast(I32))
+        load_scales(nc.sync, ws_raw, w_scales)
+        nc.sync.dma_start(out=w_raw[:].bitcast(I32), in_=w_words[0].bitcast(I32))
         nc.sync.dma_start(out=sx_c[:].bitcast(I32), in_=sx_words[0].rearrange("p n t -> p (n t)").bitcast(I32))
+        load_scales(nc.sync, sx_s, sx_scales, range(3, 4))
+        nc.sync.dma_start(out=rs_t[:], in_=rs.rearrange("(h p) n -> p h n", p=P))
         nc.sync.dma_start(out=wb_c[:].bitcast(I32), in_=wb_words[0].rearrange("p n t -> p (n t)").bitcast(I32))
         load_scales(nc.sync, wb_s, wb_scales)
-        nc.sync.dma_start(out=rs_t[:], in_=rs.rearrange("(h p) n -> p h n", p=P))
 
         ha = keep.tile([P, (LAG + J) * PACK], F32, name="ha")
         zeros = keep.tile([P, LAG * PACK], F32, name="zeros")
@@ -102,11 +96,15 @@ def tile_list_sum_largerpicks_own_lagged_rowabove_kernel(
 
         def pick_pair(first, cols, b_on_vector, tag_a, tag_b):
             width = cols.stop - cols.start
-            pick_a = keep.tile([P, 2, width], F32, name="a" + tag_a, tag=tag_a, align_bytes=64)
-            pick_b = keep.tile([P, 2, width], F32, name="b" + tag_b, tag=tag_b, align_bytes=64)
+            pick_a = keep.tile([P, 2, width], F32, name="a%d_%d" % (first, cols.start), tag=tag_a, align_bytes=64)
+            pick_b = keep.tile([P, 2, width], F32, name="b%d_%d" % (first, cols.start), tag=tag_b, align_bytes=64)
             for t in range(2):
-                gather(False, pick_a[:, t, :], list_a, first + t, cols)
-                gather(b_on_vector, pick_b[:, t, :], list_b, first + t, cols)
+                if first + t == 1:
+                    gather(False, pick_a[:, t, 0:H], list_a, 1, slice(0, H))
+                    gather(True, pick_a[:, t, H:J], list_a, 1, slice(H, J))
+                else:
+                    gather(False, pick_a[:, t, :], list_a, first + t, cols)
+                gather(b_on_vector[t], pick_b[:, t, :], list_b, first + t, cols)
             nc.vector.tensor_tensor(larger[:, first : first + 2, cols], pick_a[:], pick_b[:], ALU.max)
 
         u_c = [keep.tile([P, H], U32, name="u_c%d" % h, align_bytes=64) for h in range(HALVES)]
@@ -124,73 +122,69 @@ def tile_list_sum_largerpicks_own_lagged_rowabove_kernel(
             )
             nc.vector.quantize_mx(out=u_c[h][:].bitcast(E4M3), scales=u_s[h][:], in_=u_b[:].rearrange("p j t -> p (j t)"))
 
-        pick_pair(0, slice(0, J), True, "a01", "b01")
-        pick_pair(2, slice(0, H), True, "a23", "b23")
-        make_u(0)
-        nc.scalar.copy(*dealt(w_raw[:], w_c[:], 8))
-        nc.scalar.copy(*dealt(w2_raw[:], w2_c[:], 4))
-        nc.vector.tensor_copy(*dealt(ws_raw, w_s[:], 16))
+        pick_pair(0, slice(0, J), (True, True), "a01", "b01")
         nc.vector.tensor_copy(*dealt(w2s_raw, w2_s[:], 16))
-        pick_pair(2, slice(H, J), False, "w_then_a", "w2_then_b")
+        nc.vector.tensor_copy(*dealt(ws_raw, w_s[:], 16))
+        pick_pair(2, slice(0, H), (True, True), "a23", "b23")
+        make_u(0)
+        w2_c = keep.tile([P, R], U32, name="w2_c", align_bytes=64)
+        nc.scalar.copy(*dealt(w2_raw[:], w2_c[:], 4))
+        pick_pair(2, slice(H, J), (False, False), "w2_then_a", "b23late")
+        w_c = keep.tile([P, R], U16, name="w_c", tag="x3", align_bytes=64)
+        nc.scalar.copy(*dealt(w_raw[:], w_c[:], 8))
         make_u(1)
 
+        pieces = [[(0, H)], [(0, H // 2), (H // 2, H)]]
         sums = [psum.tile([P, PACK, H], F32, name="sums%d" % h) for h in range(HALVES)]
         for h in range(HALVES):
             cols = slice(h * H, (h + 1) * H)
-            for t in range(PACK):
-                rows = slice(t * P, (t + 1) * P)
-                nc.tensor.matmul_mx(
-                    out=sums[h][:, t, :],
-                    lhsT=w2_c[:, rows].bitcast(E5M2),
-                    lhsT_scale=w2_s[:, rows],
-                    rhs=sx_c[:, cols].bitcast(E4M3),
-                    rhs_scale=sx_s[:, cols],
-                    start=(t == 0),
-                    stop=False,
+            picked = (w_c, E2M1, w_s, u_c[h][:], u_s[h][:])
+            own = (w2_c, E5M2, w2_s, sx_c[:, cols], sx_s[:, cols])
+            for i, (codes, fmt, scales, moving, moving_scales) in enumerate((own, picked)):
+                for t in range(PACK):
+                    rows = slice(t * P, (t + 1) * P)
+                    nc.tensor.matmul_mx(
+                        out=sums[h][:, t, :],
+                        lhsT=codes[:, rows].bitcast(fmt),
+                        lhsT_scale=scales[:, rows],
+                        rhs=moving.bitcast(E4M3),
+                        rhs_scale=moving_scales,
+                        start=(i == 0 and t == 0),
+                        stop=(i == 1 and t == PACK - 1),
+                    )
+            for lo, hi in pieces[h]:
+                now = ha[:, (h * H + lo + LAG) * PACK : (h * H + hi + LAG) * PACK]
+                nc.scalar.activation(
+                    now.rearrange("p (j t) -> p j t", t=PACK), sums[h][:, :, lo:hi].rearrange("p t j -> p j t"), ACT.Relu
                 )
-            for t in range(PACK):
-                rows = slice(t * P, (t + 1) * P)
-                nc.tensor.matmul_mx(
-                    out=sums[h][:, t, :],
-                    lhsT=w_c[:, rows].bitcast(E2M1),
-                    lhsT_scale=w_s[:, rows],
-                    rhs=u_c[h][:].bitcast(E4M3),
-                    rhs_scale=u_s[h][:],
-                    start=False,
-                    stop=(t == PACK - 1),
-                )
-            first = h * H * PACK
-            now = ha[:, first + LAG * PACK : first + (LAG + H) * PACK]
-            nc.scalar.activation(now.rearrange("p (j t) -> p j t", t=PACK), sums[h][:].rearrange("p t j -> p j t"), ACT.Relu)
         hid_b = [keep.tile([P, H * PACK], BF16, name="hid_b%d" % h, align_bytes=64) for h in range(HALVES)]
         hid_c = [keep.tile([P, H], U32, name="hid_c%d" % h, align_bytes=64) for h in range(HALVES)]
         hid_s = [keep.tile([P, H], U8, name="hid_s%d" % h, align_bytes=64) for h in range(HALVES)]
-        prod = [[psum.tile([P, N], F32, name="prod%d%d" % (h, r)) for r in range(2)] for h in range(HALVES)]
-        less = keep.tile([P, HALVES, N], F32, name="less")
+        prod = [psum.tile([P, N], F32, name="prod%d" % h) for h in range(HALVES)]
         for h in range(HALVES):
-            nc.scalar.activation(less[:, h, :], rs_t[:, h, :], ACT.Copy, scale=-0.3)
-        for h in range(HALVES):
-            first = h * H * PACK
-            now = ha[:, first + LAG * PACK : first + (LAG + H) * PACK]
-            before = ha[:, first : first + H * PACK]
-            nc.vector.scalar_tensor_tensor(hid_b[h][:], before, -0.5, now, ALU.mult, ALU.add)
-            nc.vector.quantize_mx(out=hid_c[h][:].bitcast(E5M2), scales=hid_s[h][:], in_=hid_b[h][:])
-            for bank in prod[h]:
-                nc.tensor.matmul_mx(
-                    out=bank[:],
-                    lhsT=hid_c[h][:].bitcast(E5M2),
-                    lhsT_scale=hid_s[h][:],
-                    rhs=wb_c[:].bitcast(E5M2),
-                    rhs_scale=wb_s,
-                    start=True,
-                    stop=True,
+            for lo, hi in pieces[h]:
+                now = ha[:, (h * H + lo + LAG) * PACK : (h * H + hi + LAG) * PACK]
+                before = ha[:, (h * H + lo) * PACK : (h * H + hi) * PACK]
+                nc.vector.scalar_tensor_tensor(hid_b[h][:, lo * PACK : hi * PACK], before, -0.5, now, ALU.mult, ALU.add)
+            for lo, hi in pieces[h]:
+                nc.vector.quantize_mx(
+                    out=hid_c[h][:, lo:hi].bitcast(E5M2), scales=hid_s[h][:, lo:hi], in_=hid_b[h][:, lo * PACK : hi * PACK]
                 )
+            nc.tensor.matmul_mx(
+                out=prod[h][:],
+                lhsT=hid_c[h][:].bitcast(E5M2),
+                lhsT_scale=hid_s[h][:],
+                rhs=wb_c[:].bitcast(E5M2),
+                rhs_scale=wb_s,
+                start=True,
+                stop=True,
+            )
         for h in range(HALVES):
             size = keep.tile([P, N], F32, name="size%d" % h)
             mean = keep.tile([P, 1], F32, name="mean%d" % h)
             taken = keep.tile([P, N], F32, name="taken%d" % h)
             result = keep.tile([P, N], F32, name="result%d" % h)
-            nc.scalar.activation(size[:], prod[h][0][:], ACT.Abs, scale=1.0 / N, accum_out=mean[:])
-            nc.vector.tensor_tensor(taken[:], prod[h][1][:], less[:, h, :], ALU.add)
-            nc.vector.scalar_tensor_tensor(result[:], taken[:], mean[:], less[:, h, :], ALU.subtract, ALU.max)
+            nc.scalar.activation(size[:], prod[h][:], ACT.Abs, scale=1.0 / N, accum_out=mean[:])
+            nc.vector.tensor_scalar(taken[:], rs_t[:, h, :], 0.3, mean[:], ALU.mult, ALU.add)
+            nc.vector.scalar_tensor_tensor(result[:], prod[h][:], mean[:], taken[:], ALU.max, ALU.subtract)
             nc.sync.dma_start(out=out[h * H : (h + 1) * H, :], in_=result[:])

@@ -20,19 +20,26 @@ ACT = mybir.ActivationFunctionType
 P = 128
 PACK = 4
 H = 128
-HALVES = J // H
 LAG = 2
+LINE = 16
+QUADRANTS = range(4)
+FIRST, SECOND, ALL = slice(0, H), slice(H, J), slice(0, J)
 
 
-def load_scales(queue, plane, scales, quadrants=range(4)):
+def load_scale_rows(queue, plane, scales, quadrants):
     for q in quadrants:
         queue.dma_start(out=plane[32 * q : 32 * q + 4, :].bitcast(I32), in_=scales[0, 4 * q : 4 * q + 4, :].bitcast(I32))
 
 
-def dealt(src, dst, run):
+def load_words(nc, codes, words):
+    nc.sync.dma_start(out=codes.bitcast(I32), in_=words[0].rearrange("p n t -> p (n t)").bitcast(I32))
+
+
+def dealing_views(dealt, raw, element_bytes):
+    run = LINE // element_bytes
     return (
-        dst.rearrange("p (t c i) -> p c t i", t=PACK, i=run),
-        src.rearrange("p (c i t) -> p c t i", t=PACK, i=run),
+        dealt.rearrange("p (t c i) -> p c t i", t=PACK, i=run),
+        raw.rearrange("p (c i t) -> p c t i", t=PACK, i=run),
     )
 
 
@@ -44,147 +51,162 @@ def tile_list_sum_largerpicks_own_lagged_rowabove_kernel(
         keep = ctx.enter_context(tc.tile_pool(name="keep", bufs=1))
         psum = ctx.enter_context(tc.psum_pool(name="psum", bufs=1))
 
+        def sbuf(name, shape, dtype, after=None):
+            return keep.tile(shape, dtype, name=name, tag=after or name, align_bytes=64)[:]
+
         list_a = keep.tile([P, J // 16], U16, name="list_a")
         list_b = keep.tile([P, J // 16], U16, name="list_b")
-        planes = [keep.tile([P, T], F32, name="x%d" % t, tag="x%d" % t, align_bytes=64)[:] for t in range(PACK)]
-        fk_t = keep.tile([P, PACK], F32, name="fk_t")
-        w_raw = keep.tile([P, R], U16, name="w_raw", align_bytes=64)
-        w2_raw = keep.tile([P, R], U32, name="w2_raw", tag="w2_then_a", align_bytes=64)
-        ws_raw = keep.tile([P, R], U8, name="ws_raw", tag="w2s_then_u", align_bytes=64)[:]
-        w2s_raw = keep.tile([P, R], U8, name="w2s_raw", align_bytes=64)[:]
-        sx_s = keep.tile([P, J], U8, name="sx_s", align_bytes=64)[:]
-        wb_s = keep.tile([P, N], U8, name="wb_s", align_bytes=64)[:]
-        w_s = keep.tile([P, R], U8, name="w_s", align_bytes=64)
-        w2_s = keep.tile([P, R], U8, name="w2_s", align_bytes=64)
-        sx_c = keep.tile([P, J], U32, name="sx_c", align_bytes=64)
-        wb_c = keep.tile([P, N], U32, name="wb_c", align_bytes=64)
-        rs_t = keep.tile([P, HALVES, N], F32, name="rs_t")
+        planes = [sbuf("plane%d" % t, [P, T], F32) for t in range(PACK)]
+        factors = sbuf("factors", [P, PACK], F32)
+        w_raw = sbuf("w_raw", [P, R], U16)
+        w2_raw = sbuf("w2_raw", [P, R], U32)
+        sx_codes = sbuf("sx_codes", [P, J], U32)
+        wb_codes = sbuf("wb_codes", [P, N], U32)
+        residual = sbuf("residual", [P, J // H, N], F32)
+        w2_scales_raw = sbuf("w2_scales_raw", [P, R], U8)
+        w_scales_raw = sbuf("w_scales_raw", [P, R], U8)
+        sx_scale = sbuf("sx_scale", [P, J], U8)
+        wb_scale = sbuf("wb_scale", [P, N], U8)
 
-        for plane in (w2s_raw, sx_s, ws_raw, wb_s):
-            nc.vector.memset(plane.bitcast(I32), 0)
-        x_rows = xf.rearrange("(p t) c -> p t c", t=PACK)
-        nc.sync.dma_start(out=planes[0], in_=x_rows[:, 0, :])
+        for scale_tile in (w2_scales_raw, sx_scale, w_scales_raw, wb_scale):
+            nc.vector.memset(scale_tile.bitcast(I32), 0)
+
         nc.sync.dma_start(list_a[:], offs)
         nc.sync.dma_start(list_b[:], offs2)
-        for t in range(1, PACK):
+        x_rows = xf.rearrange("(p t) c -> p t c", t=PACK)
+        for t in range(PACK):
             nc.sync.dma_start(out=planes[t], in_=x_rows[:, t, :])
-        nc.gpsimd.dma_start(out=fk_t[:], in_=fk.rearrange("(p t) o -> p (t o)", t=PACK))
-        load_scales(nc.gpsimd, sx_s, sx_scales, range(0, 3))
-        load_scales(nc.sync, w2s_raw, w2_scales)
-        nc.sync.dma_start(out=w2_raw[:].bitcast(I32), in_=w2_words[0].rearrange("p n t -> p (n t)").bitcast(I32))
-        load_scales(nc.sync, ws_raw, w_scales)
-        nc.sync.dma_start(out=w_raw[:].bitcast(I32), in_=w_words[0].bitcast(I32))
-        nc.sync.dma_start(out=sx_c[:].bitcast(I32), in_=sx_words[0].rearrange("p n t -> p (n t)").bitcast(I32))
-        load_scales(nc.sync, sx_s, sx_scales, range(3, 4))
-        nc.sync.dma_start(out=rs_t[:], in_=rs.rearrange("(h p) n -> p h n", p=P))
-        nc.sync.dma_start(out=wb_c[:].bitcast(I32), in_=wb_words[0].rearrange("p n t -> p (n t)").bitcast(I32))
-        load_scales(nc.sync, wb_s, wb_scales)
+        nc.gpsimd.dma_start(out=factors, in_=fk.rearrange("(p t) o -> p (t o)", t=PACK))
+        load_scale_rows(nc.gpsimd, sx_scale, sx_scales, QUADRANTS[:3])
+        load_scale_rows(nc.sync, w2_scales_raw, w2_scales, QUADRANTS)
+        load_words(nc, w2_raw, w2_words)
+        load_scale_rows(nc.sync, w_scales_raw, w_scales, QUADRANTS)
+        nc.sync.dma_start(out=w_raw.bitcast(I32), in_=w_words[0].bitcast(I32))
+        load_words(nc, sx_codes, sx_words)
+        load_scale_rows(nc.sync, sx_scale, sx_scales, QUADRANTS[3:])
+        nc.sync.dma_start(out=residual, in_=rs.rearrange("(h p) n -> p h n", p=P))
+        load_words(nc, wb_codes, wb_words)
+        load_scale_rows(nc.sync, wb_scale, wb_scales, QUADRANTS)
 
-        ha = keep.tile([P, (LAG + J) * PACK], F32, name="ha")
-        zeros = keep.tile([P, LAG * PACK], F32, name="zeros")
-        nc.vector.memset(zeros[:], 0.0)
-        nc.scalar.activation(ha[:, 0 : LAG * PACK], zeros[:], ACT.Relu)
+        ha = sbuf("ha", [P, (LAG + J) * PACK], F32)
+        zeros = sbuf("zeros", [P, LAG * PACK], F32)
+        nc.vector.memset(zeros, 0.0)
+        nc.scalar.activation(ha[:, 0 : LAG * PACK], zeros, ACT.Relu)
 
-        larger = keep.tile([P, PACK, J], F32, name="larger")
-
-        def gather(on_vector, pick, offsets, t, cols):
-            window = planes[t].indirect(offsets[:, cols.start // 16 : cols.stop // 16])
-            if on_vector:
+        def gather(engine, pick, offsets, t, slots):
+            window = planes[t].indirect(offsets[:, slots.start // 16 : slots.stop // 16])
+            if engine == "vector":
                 nc.vector.tensor_copy(pick, window)
             else:
                 nc.scalar.activation(pick, window, ACT.Copy)
 
-        def pick_pair(first, cols, b_on_vector, tag_a, tag_b):
-            width = cols.stop - cols.start
-            pick_a = keep.tile([P, 2, width], F32, name="a%d_%d" % (first, cols.start), tag=tag_a, align_bytes=64)
-            pick_b = keep.tile([P, 2, width], F32, name="b%d_%d" % (first, cols.start), tag=tag_b, align_bytes=64)
-            for t in range(2):
-                if first + t == 1:
-                    gather(False, pick_a[:, t, 0:H], list_a, 1, slice(0, H))
-                    gather(True, pick_a[:, t, H:J], list_a, 1, slice(H, J))
-                else:
-                    gather(False, pick_a[:, t, :], list_a, first + t, cols)
-                gather(b_on_vector[t], pick_b[:, t, :], list_b, first + t, cols)
-            nc.vector.tensor_tensor(larger[:, first : first + 2, cols], pick_a[:], pick_b[:], ALU.max)
+        larger = sbuf("larger", [P, PACK, J], F32)
 
-        u_c = [keep.tile([P, H], U32, name="u_c%d" % h, align_bytes=64) for h in range(HALVES)]
-        u_s = [keep.tile([P, H], U8, name="u_s%d" % h, align_bytes=64) for h in range(HALVES)]
-        fk_wide = fk_t[:].unsqueeze(1).unsqueeze(3).to_broadcast([P, H // 4, PACK, 4])
+        def keep_larger(pair, slots, pick_a, pick_b):
+            nc.vector.tensor_tensor(larger[:, 2 * pair : 2 * pair + 2, slots], pick_a, pick_b, ALU.max)
 
-        def make_u(h):
-            cols = slice(h * H, (h + 1) * H)
-            u_b = keep.tile([P, H, PACK], BF16, name="u_b%d" % h, tag=("u0", "w2s_then_u")[h], align_bytes=64)
+        early_a = sbuf("early_a", [P, 2, J], F32)
+        early_b = sbuf("early_b", [P, 2, J], F32)
+        gather("scalar", early_a[:, 0, :], list_a, 0, ALL)
+        gather("vector", early_b[:, 0, :], list_b, 0, ALL)
+        gather("scalar", early_a[:, 1, FIRST], list_a, 1, FIRST)
+        gather("vector", early_a[:, 1, SECOND], list_a, 1, SECOND)
+        gather("vector", early_b[:, 1, :], list_b, 1, ALL)
+        keep_larger(0, ALL, early_a, early_b)
+
+        w2_scale = sbuf("w2_scale", [P, R], U8)
+        w_scale = sbuf("w_scale", [P, R], U8)
+        nc.vector.tensor_copy(*dealing_views(w2_scale, w2_scales_raw, 1))
+        nc.vector.tensor_copy(*dealing_views(w_scale, w_scales_raw, 1))
+
+        def pick_late_planes(slots, engine_b, pick_a, pick_b):
+            for i in range(2):
+                gather("scalar", pick_a[:, i, :], list_a, 2 + i, slots)
+                gather(engine_b, pick_b[:, i, :], list_b, 2 + i, slots)
+            keep_larger(1, slots, pick_a, pick_b)
+
+        run = LINE // 4
+        factors_wide = factors.unsqueeze(1).unsqueeze(3).to_broadcast([P, H // run, PACK, run])
+
+        def quantise_u(slots, rounded, codes, scale):
             nc.vector.tensor_tensor(
-                u_b[:].rearrange("p (c i) t -> p c t i", i=4),
-                larger[:, :, cols].rearrange("p t (c i) -> p c t i", i=4),
-                fk_wide,
+                rounded.rearrange("p (c i) t -> p c t i", i=run),
+                larger[:, :, slots].rearrange("p t (c i) -> p c t i", i=run),
+                factors_wide,
                 ALU.mult,
             )
-            nc.vector.quantize_mx(out=u_c[h][:].bitcast(E4M3), scales=u_s[h][:], in_=u_b[:].rearrange("p j t -> p (j t)"))
+            nc.vector.quantize_mx(out=codes.bitcast(E4M3), scales=scale, in_=rounded.rearrange("p j t -> p (j t)"))
 
-        pick_pair(0, slice(0, J), (True, True), "a01", "b01")
-        nc.vector.tensor_copy(*dealt(w2s_raw, w2_s[:], 16))
-        nc.vector.tensor_copy(*dealt(ws_raw, w_s[:], 16))
-        pick_pair(2, slice(0, H), (True, True), "a23", "b23")
-        make_u(0)
-        w2_c = keep.tile([P, R], U32, name="w2_c", align_bytes=64)
-        nc.scalar.copy(*dealt(w2_raw[:], w2_c[:], 4))
-        pick_pair(2, slice(H, J), (False, False), "w2_then_a", "b23late")
-        w_c = keep.tile([P, R], U16, name="w_c", tag="x3", align_bytes=64)
-        nc.scalar.copy(*dealt(w_raw[:], w_c[:], 8))
-        make_u(1)
+        pick_late_planes(FIRST, "vector", sbuf("first_a", [P, 2, H], F32), sbuf("first_b", [P, 2, H], F32))
+        u_codes = [sbuf("u_codes0", [P, H], U32, after="w2_scales_raw"), sbuf("u_codes1", [P, H], U32)]
+        u_scale = [sbuf("u_scale%d" % h, [P, H], U8) for h in range(2)]
+        quantise_u(FIRST, sbuf("u_rounded0", [P, H, PACK], BF16), u_codes[0], u_scale[0])
+
+        w2_codes = sbuf("w2_codes", [P, R], U32)
+        nc.scalar.copy(*dealing_views(w2_codes, w2_raw, 4))
+        second_a = sbuf("second_a", [P, 2, H], F32, after="w2_raw")
+        pick_late_planes(SECOND, "scalar", second_a, sbuf("second_b", [P, 2, H], F32))
+        w_codes = sbuf("w_codes", [P, R], U16, after="plane3")
+        nc.scalar.copy(*dealing_views(w_codes, w_raw, 2))
+        quantise_u(SECOND, sbuf("u_rounded1", [P, H, PACK], BF16, after="w_scales_raw"), u_codes[1], u_scale[1])
 
         pieces = [[(0, H)], [(0, H // 2), (H // 2, H)]]
-        sums = [psum.tile([P, PACK, H], F32, name="sums%d" % h) for h in range(HALVES)]
-        for h in range(HALVES):
-            cols = slice(h * H, (h + 1) * H)
-            picked = (w_c, E2M1, w_s, u_c[h][:], u_s[h][:])
-            own = (w2_c, E5M2, w2_s, sx_c[:, cols], sx_s[:, cols])
-            for i, (codes, fmt, scales, moving, moving_scales) in enumerate((own, picked)):
+
+        for h, slots in enumerate((FIRST, SECOND)):
+            sums = psum.tile([P, PACK, H], F32, name="sums%d" % h)
+            own = (w2_codes, E5M2, w2_scale, sx_codes[:, slots], sx_scale[:, slots])
+            picked = (w_codes, E2M1, w_scale, u_codes[h], u_scale[h])
+            for i, (codes, fmt, scale, moving, moving_scale) in enumerate((own, picked)):
                 for t in range(PACK):
-                    rows = slice(t * P, (t + 1) * P)
+                    places = slice(t * P, (t + 1) * P)
                     nc.tensor.matmul_mx(
-                        out=sums[h][:, t, :],
-                        lhsT=codes[:, rows].bitcast(fmt),
-                        lhsT_scale=scales[:, rows],
+                        out=sums[:, t, :],
+                        lhsT=codes[:, places].bitcast(fmt),
+                        lhsT_scale=scale[:, places],
                         rhs=moving.bitcast(E4M3),
-                        rhs_scale=moving_scales,
+                        rhs_scale=moving_scale,
                         start=(i == 0 and t == 0),
                         stop=(i == 1 and t == PACK - 1),
                     )
             for lo, hi in pieces[h]:
-                now = ha[:, (h * H + lo + LAG) * PACK : (h * H + hi + LAG) * PACK]
+                now = ha[:, (LAG + slots.start + lo) * PACK : (LAG + slots.start + hi) * PACK]
                 nc.scalar.activation(
-                    now.rearrange("p (j t) -> p j t", t=PACK), sums[h][:, :, lo:hi].rearrange("p t j -> p j t"), ACT.Relu
+                    now.rearrange("p (j t) -> p j t", t=PACK), sums[:, :, lo:hi].rearrange("p t j -> p j t"), ACT.Relu
                 )
-        hid_b = [keep.tile([P, H * PACK], BF16, name="hid_b%d" % h, align_bytes=64) for h in range(HALVES)]
-        hid_c = [keep.tile([P, H], U32, name="hid_c%d" % h, align_bytes=64) for h in range(HALVES)]
-        hid_s = [keep.tile([P, H], U8, name="hid_s%d" % h, align_bytes=64) for h in range(HALVES)]
-        prod = [psum.tile([P, N], F32, name="prod%d" % h) for h in range(HALVES)]
-        for h in range(HALVES):
+
+        products = []
+        for h, slots in enumerate((FIRST, SECOND)):
+            hid_rounded = sbuf("hid_rounded%d" % h, [P, H * PACK], BF16)
+            hid_codes = sbuf("hid_codes%d" % h, [P, H], U32)
+            hid_scale = sbuf("hid_scale%d" % h, [P, H], U8)
             for lo, hi in pieces[h]:
-                now = ha[:, (h * H + lo + LAG) * PACK : (h * H + hi + LAG) * PACK]
-                before = ha[:, (h * H + lo) * PACK : (h * H + hi) * PACK]
-                nc.vector.scalar_tensor_tensor(hid_b[h][:, lo * PACK : hi * PACK], before, -0.5, now, ALU.mult, ALU.add)
+                now = ha[:, (LAG + slots.start + lo) * PACK : (LAG + slots.start + hi) * PACK]
+                before = ha[:, (slots.start + lo) * PACK : (slots.start + hi) * PACK]
+                nc.vector.scalar_tensor_tensor(hid_rounded[:, lo * PACK : hi * PACK], before, -0.5, now, ALU.mult, ALU.add)
             for lo, hi in pieces[h]:
                 nc.vector.quantize_mx(
-                    out=hid_c[h][:, lo:hi].bitcast(E5M2), scales=hid_s[h][:, lo:hi], in_=hid_b[h][:, lo * PACK : hi * PACK]
+                    out=hid_codes[:, lo:hi].bitcast(E5M2),
+                    scales=hid_scale[:, lo:hi],
+                    in_=hid_rounded[:, lo * PACK : hi * PACK],
                 )
+            product = psum.tile([P, N], F32, name="product%d" % h)
             nc.tensor.matmul_mx(
-                out=prod[h][:],
-                lhsT=hid_c[h][:].bitcast(E5M2),
-                lhsT_scale=hid_s[h][:],
-                rhs=wb_c[:].bitcast(E5M2),
-                rhs_scale=wb_s,
+                out=product[:],
+                lhsT=hid_codes.bitcast(E5M2),
+                lhsT_scale=hid_scale,
+                rhs=wb_codes.bitcast(E5M2),
+                rhs_scale=wb_scale,
                 start=True,
                 stop=True,
             )
-        for h in range(HALVES):
-            size = keep.tile([P, N], F32, name="size%d" % h)
-            mean = keep.tile([P, 1], F32, name="mean%d" % h)
-            taken = keep.tile([P, N], F32, name="taken%d" % h)
-            result = keep.tile([P, N], F32, name="result%d" % h)
-            nc.scalar.activation(size[:], prod[h][:], ACT.Abs, scale=1.0 / N, accum_out=mean[:])
-            nc.vector.tensor_scalar(taken[:], rs_t[:, h, :], 0.3, mean[:], ALU.mult, ALU.add)
-            nc.vector.scalar_tensor_tensor(result[:], prod[h][:], mean[:], taken[:], ALU.max, ALU.subtract)
-            nc.sync.dma_start(out=out[h * H : (h + 1) * H, :], in_=result[:])
+            products.append(product)
+
+        for h, slots in enumerate((FIRST, SECOND)):
+            magnitude = sbuf("magnitude%d" % h, [P, N], F32)
+            mean = sbuf("mean%d" % h, [P, 1], F32)
+            taken_off = sbuf("taken_off%d" % h, [P, N], F32)
+            result = sbuf("result%d" % h, [P, N], F32)
+            nc.scalar.activation(magnitude, products[h][:], ACT.Abs, scale=1.0 / N, accum_out=mean)
+            nc.vector.tensor_scalar(taken_off, residual[:, h, :], 0.3, mean, ALU.mult, ALU.add)
+            nc.vector.scalar_tensor_tensor(result, products[h][:], mean, taken_off, ALU.max, ALU.subtract)
+            nc.sync.dma_start(out=out[slots, :], in_=result)

from contextlib import ExitStack

import concourse.mybir as mybir

K, T, J, R, F, N = 512, 512, 256, 512, 512, 256
FLOPS = 2 * K * R * J + 2 * F * R * J + 2 * R * J * N

F32 = mybir.dt.float32
BF16 = mybir.dt.bfloat16
I32 = mybir.dt.int32
U32 = mybir.dt.uint32
U16 = mybir.dt.uint16
U8 = mybir.dt.uint8
E4M3 = mybir.dt.float8_e4m3fn_x4
E5M2 = mybir.dt.float8_e5m2_x4
E2M1 = mybir.dt.float4_e2m1fn_x4
ALU = mybir.AluOpType
ACT = mybir.ActivationFunctionType

P = 128
PACK = 4
H = 128
LAG = 2
LINE = 16
QUADRANTS = range(4)
FIRST, SECOND, ALL = slice(0, H), slice(H, J), slice(0, J)


def load_scale_rows(queue, plane, scales, quadrants):
    for q in quadrants:
        queue.dma_start(out=plane[32 * q : 32 * q + 4, :].bitcast(I32), in_=scales[0, 4 * q : 4 * q + 4, :].bitcast(I32))


def load_words(nc, codes, words):
    nc.sync.dma_start(out=codes.bitcast(I32), in_=words[0].rearrange("p n t -> p (n t)").bitcast(I32))


def dealing_views(dealt, raw, element_bytes):
    run = LINE // element_bytes
    return (
        dealt.rearrange("p (t c i) -> p c t i", t=PACK, i=run),
        raw.rearrange("p (c i t) -> p c t i", t=PACK, i=run),
    )


def tile_list_sum_largerpicks_own_lagged_rowabove_kernel(
    tc, xf, fk, w_words, w_scales, sx_words, sx_scales, w2_words, w2_scales, wb_words, wb_scales, rs, offs, offs2, out
):
    nc = tc.nc
    with ExitStack() as ctx:
        keep = ctx.enter_context(tc.tile_pool(name="keep", bufs=1))
        psum = ctx.enter_context(tc.psum_pool(name="psum", bufs=1))

        def sbuf(name, shape, dtype, after=None):
            return keep.tile(shape, dtype, name=name, tag=after or name, align_bytes=64)[:]

        list_a = keep.tile([P, J // 16], U16, name="list_a")
        list_b = keep.tile([P, J // 16], U16, name="list_b")
        planes = [sbuf("plane%d" % t, [P, T], F32) for t in range(PACK)]
        factors = sbuf("factors", [P, PACK], F32)
        w_raw = sbuf("w_raw", [P, R], U16)
        w2_raw = sbuf("w2_raw", [P, R], U32)
        sx_codes = sbuf("sx_codes", [P, J], U32)
        wb_codes = sbuf("wb_codes", [P, N], U32)
        residual = sbuf("residual", [P, J // H, N], F32)
        w2_scales_raw = sbuf("w2_scales_raw", [P, R], U8)
        w_scales_raw = sbuf("w_scales_raw", [P, R], U8)
        sx_scale = sbuf("sx_scale", [P, J], U8)
        wb_scale = sbuf("wb_scale", [P, N], U8)

        for scale_tile in (w2_scales_raw, sx_scale, w_scales_raw, wb_scale):
            nc.vector.memset(scale_tile.bitcast(I32), 0)

        nc.sync.dma_start(list_a[:], offs)
        nc.sync.dma_start(list_b[:], offs2)
        x_rows = xf.rearrange("(p t) c -> p t c", t=PACK)
        for t in range(PACK):
            nc.sync.dma_start(out=planes[t], in_=x_rows[:, t, :])
        nc.gpsimd.dma_start(out=factors, in_=fk.rearrange("(p t) o -> p (t o)", t=PACK))
        load_scale_rows(nc.gpsimd, sx_scale, sx_scales, QUADRANTS[:3])
        load_scale_rows(nc.sync, w2_scales_raw, w2_scales, QUADRANTS)
        load_words(nc, w2_raw, w2_words)
        load_scale_rows(nc.sync, w_scales_raw, w_scales, QUADRANTS)
        nc.sync.dma_start(out=w_raw.bitcast(I32), in_=w_words[0].bitcast(I32))
        load_words(nc, sx_codes, sx_words)
        load_scale_rows(nc.sync, sx_scale, sx_scales, QUADRANTS[3:])
        nc.sync.dma_start(out=residual, in_=rs.rearrange("(h p) n -> p h n", p=P))
        load_words(nc, wb_codes, wb_words)
        load_scale_rows(nc.sync, wb_scale, wb_scales, QUADRANTS)

        ha = sbuf("ha", [P, (LAG + J) * PACK], F32)
        zeros = sbuf("zeros", [P, LAG * PACK], F32)
        nc.vector.memset(zeros, 0.0)
        nc.scalar.activation(ha[:, 0 : LAG * PACK], zeros, ACT.Relu)

        def gather(engine, pick, offsets, t, slots):
            window = planes[t].indirect(offsets[:, slots.start // 16 : slots.stop // 16])
            if engine == "vector":
                nc.vector.tensor_copy(pick, window)
            else:
                nc.scalar.activation(pick, window, ACT.Copy)

        larger = sbuf("larger", [P, PACK, J], F32)

        def keep_larger(pair, slots, pick_a, pick_b):
            nc.vector.tensor_tensor(larger[:, 2 * pair : 2 * pair + 2, slots], pick_a, pick_b, ALU.max)

        early_a = sbuf("early_a", [P, 2, J], F32)
        early_b = sbuf("early_b", [P, 2, J], F32)
        gather("scalar", early_a[:, 0, :], list_a, 0, ALL)
        gather("vector", early_b[:, 0, :], list_b, 0, ALL)
        gather("scalar", early_a[:, 1, FIRST], list_a, 1, FIRST)
        gather("vector", early_a[:, 1, SECOND], list_a, 1, SECOND)
        gather("vector", early_b[:, 1, :], list_b, 1, ALL)
        keep_larger(0, ALL, early_a, early_b)

        w2_scale = sbuf("w2_scale", [P, R], U8)
        w_scale = sbuf("w_scale", [P, R], U8)
        nc.vector.tensor_copy(*dealing_views(w2_scale, w2_scales_raw, 1))
        nc.vector.tensor_copy(*dealing_views(w_scale, w_scales_raw, 1))

        def pick_late_planes(slots, engine_b, pick_a, pick_b):
            for i in range(2):
                gather("scalar", pick_a[:, i, :], list_a, 2 + i, slots)
                gather(engine_b, pick_b[:, i, :], list_b, 2 + i, slots)
            keep_larger(1, slots, pick_a, pick_b)

        run = LINE // 4
        factors_wide = factors.unsqueeze(1).unsqueeze(3).to_broadcast([P, H // run, PACK, run])

        def quantise_u(slots, rounded, codes, scale):
            nc.vector.tensor_tensor(
                rounded.rearrange("p (c i) t -> p c t i", i=run),
                larger[:, :, slots].rearrange("p t (c i) -> p c t i", i=run),
                factors_wide,
                ALU.mult,
            )
            nc.vector.quantize_mx(out=codes.bitcast(E4M3), scales=scale, in_=rounded.rearrange("p j t -> p (j t)"))

        pick_late_planes(FIRST, "vector", sbuf("first_a", [P, 2, H], F32), sbuf("first_b", [P, 2, H], F32))
        u_codes = [sbuf("u_codes0", [P, H], U32, after="w2_scales_raw"), sbuf("u_codes1", [P, H], U32)]
        u_scale = [sbuf("u_scale%d" % h, [P, H], U8) for h in range(2)]
        quantise_u(FIRST, sbuf("u_rounded0", [P, H, PACK], BF16), u_codes[0], u_scale[0])

        w2_codes = sbuf("w2_codes", [P, R], U32)
        nc.scalar.copy(*dealing_views(w2_codes, w2_raw, 4))
        second_a = sbuf("second_a", [P, 2, H], F32, after="w2_raw")
        pick_late_planes(SECOND, "scalar", second_a, sbuf("second_b", [P, 2, H], F32))
        w_codes = sbuf("w_codes", [P, R], U16, after="plane3")
        nc.scalar.copy(*dealing_views(w_codes, w_raw, 2))
        quantise_u(SECOND, sbuf("u_rounded1", [P, H, PACK], BF16, after="w_scales_raw"), u_codes[1], u_scale[1])

        pieces = [[(0, H)], [(0, H // 2), (H // 2, H)]]

        for h, slots in enumerate((FIRST, SECOND)):
            sums = psum.tile([P, PACK, H], F32, name="sums%d" % h)
            own = (w2_codes, E5M2, w2_scale, sx_codes[:, slots], sx_scale[:, slots])
            picked = (w_codes, E2M1, w_scale, u_codes[h], u_scale[h])
            for i, (codes, fmt, scale, moving, moving_scale) in enumerate((own, picked)):
                for t in range(PACK):
                    places = slice(t * P, (t + 1) * P)
                    nc.tensor.matmul_mx(
                        out=sums[:, t, :],
                        lhsT=codes[:, places].bitcast(fmt),
                        lhsT_scale=scale[:, places],
                        rhs=moving.bitcast(E4M3),
                        rhs_scale=moving_scale,
                        start=(i == 0 and t == 0),
                        stop=(i == 1 and t == PACK - 1),
                    )
            for lo, hi in pieces[h]:
                now = ha[:, (LAG + slots.start + lo) * PACK : (LAG + slots.start + hi) * PACK]
                nc.scalar.activation(
                    now.rearrange("p (j t) -> p j t", t=PACK), sums[:, :, lo:hi].rearrange("p t j -> p j t"), ACT.Relu
                )

        products = []
        for h, slots in enumerate((FIRST, SECOND)):
            hid_rounded = sbuf("hid_rounded%d" % h, [P, H * PACK], BF16)
            hid_codes = sbuf("hid_codes%d" % h, [P, H], U32)
            hid_scale = sbuf("hid_scale%d" % h, [P, H], U8)
            for lo, hi in pieces[h]:
                now = ha[:, (LAG + slots.start + lo) * PACK : (LAG + slots.start + hi) * PACK]
                before = ha[:, (slots.start + lo) * PACK : (slots.start + hi) * PACK]
                nc.vector.scalar_tensor_tensor(hid_rounded[:, lo * PACK : hi * PACK], before, -0.5, now, ALU.mult, ALU.add)
            for lo, hi in pieces[h]:
                nc.vector.quantize_mx(
                    out=hid_codes[:, lo:hi].bitcast(E5M2),
                    scales=hid_scale[:, lo:hi],
                    in_=hid_rounded[:, lo * PACK : hi * PACK],
                )
            product = psum.tile([P, N], F32, name="product%d" % h)
            nc.tensor.matmul_mx(
                out=product[:],
                lhsT=hid_codes.bitcast(E5M2),
                lhsT_scale=hid_scale,
                rhs=wb_codes.bitcast(E5M2),
                rhs_scale=wb_scale,
                start=True,
                stop=True,
            )
            products.append(product)

        for h, slots in enumerate((FIRST, SECOND)):
            magnitude = sbuf("magnitude%d" % h, [P, N], F32)
            mean = sbuf("mean%d" % h, [P, 1], F32)
            taken_off = sbuf("taken_off%d" % h, [P, N], F32)
            result = sbuf("result%d" % h, [P, N], F32)
            nc.scalar.activation(magnitude, products[h][:], ACT.Abs, scale=1.0 / N, accum_out=mean)
            nc.vector.tensor_scalar(taken_off, residual[:, h, :], 0.3, mean, ALU.mult, ALU.add)
            nc.vector.scalar_tensor_tensor(result, products[h][:], mean, taken_off, ALU.max, ALU.subtract)
            nc.sync.dma_start(out=out[slots, :], in_=result)
